import numpy as np
import ml_dtypes


def mxq(x, axis, fmt="e4m3"):
    dtype, down = {"e4m3": (ml_dtypes.float8_e4m3fn, 7), "e5m2": (ml_dtypes.float8_e5m2, 14)}[fmt]
    v = np.moveaxis(np.asarray(x, np.float32).astype(ml_dtypes.bfloat16).astype(np.float64), axis, -1)
    blocks = v.reshape(v.shape[:-1] + (-1, 32))
    amax = np.abs(blocks).max(-1, keepdims=True)
    byte = np.maximum(np.where(amax > 0, np.frexp(amax)[1] - 1 + 127, 0) - down, 1)
    scale = np.exp2(byte - 127.0)
    codes = (blocks / scale).astype(np.float32).astype(dtype).astype(np.float64)
    return np.moveaxis((codes * scale).reshape(v.shape), -1, axis)


WIDE = False


def mx_kscale(k):
    if not WIDE:
        return np.ones(k)
    levels = np.array([24, -24, 12, -12, 0])
    if k % 512:
        return np.exp2(np.random.permutation(np.resize(levels, k // 32))).repeat(32)
    a = np.empty((k // 512, 16))
    for p in range(k // 512):
        a[p, :8] = np.random.permutation(np.resize(levels, 8))
        for g in range(8):
            far = levels[np.abs(levels - a[p, g]) >= 10]
            a[p, g + 8] = far[np.random.randint(len(far))]
    return np.exp2(a.ravel()).repeat(32)


def f64(x):
    return np.asarray(x).astype(np.float64)


def striped(idx):
    return np.tile(idx.reshape(-1, 16).T, (8, 1)).astype(np.uint16)


def unstriped(offs):
    return offs[:16].T.reshape(-1).astype(np.int64)


E2M1 = np.array([0.0, 0.5, 1.0, 1.5, 2.0, 3.0, 4.0, 6.0, -0.0, -0.5, -1.0, -1.5, -2.0, -3.0, -4.0, -6.0])


def pack_weight(w, fmt):
    k, n = w.shape
    w = f64(np.asarray(w, np.float32).astype(ml_dtypes.bfloat16)).reshape(k // 32, 32, n)
    amax = np.abs(w).max(1)
    if fmt == "e4m3":
        byte = np.frexp(amax)[1] - 1 + 127 - 7
    else:
        mant, ex = np.frexp(amax / 6.0)
        byte = np.where(mant > 0.5, ex, ex - 1) + 127
    byte = np.clip(np.where(amax > 0, byte, 1), 1, 254)
    scaled = (w * np.exp2(127.0 - byte)[:, None, :]).reshape(k, n).astype(np.float32)
    by_word = np.ascontiguousarray(scaled.reshape(k // 512, 128, 4, n).transpose(0, 1, 3, 2))
    if fmt == "e4m3":
        words = by_word.astype(ml_dtypes.float8_e4m3fn).view(np.uint8)
    else:
        c = by_word.astype(ml_dtypes.float4_e2m1fn).view(np.uint8) & 0xF
        words = (c[..., 0::2] | (c[..., 1::2] << 4)).reshape(k // 512, 128, 2 * n)
    return np.ascontiguousarray(words), np.ascontiguousarray(byte.astype(np.uint8).reshape(k // 512, 16, n))


def unpack_weight(words, scales, fmt):
    g, _, n = scales.shape
    words = np.ascontiguousarray(words).reshape(g, 128, n, -1)
    if fmt == "e4m3":
        vals = words.view(ml_dtypes.float8_e4m3fn).astype(np.float64)
    else:
        nib = np.empty((g, 128, n, 4), np.uint8)
        nib[..., 0::2] = words & 0xF
        nib[..., 1::2] = words >> 4
        vals = E2M1[nib]
    vals = vals * np.repeat(np.exp2(scales.astype(np.float64) - 127.0), 8, axis=1)[..., None]
    return vals.transpose(0, 1, 3, 2).reshape(g * 512, n)


def planes(y):
    n, m = y.shape
    v = y.astype(np.float32).astype(ml_dtypes.bfloat16).astype(np.float64).reshape(n // 32, 32, m)
    top = np.abs(v).max(1)
    byte = np.clip(np.where(top > 0, np.frexp(top)[1] - 1 + 127 - 7, 1), 1, 254)
    codes = (v * np.exp2(127.0 - byte)[:, None, :]).reshape(n, m).astype(np.float32).astype(ml_dtypes.float8_e4m3fn).view(np.uint8)
    words = codes.reshape(n // 512, 128, 4, m).transpose(0, 1, 3, 2)
    return np.ascontiguousarray(words), np.ascontiguousarray(byte.astype(np.uint8).reshape(n // 512, 16, m))


def sigm(f):
    return 1.0 / (1.0 + np.exp(-np.maximum(f, -700.0)))


K, N, T, J = 512, 512, 2048, 1024


def setup_inputs():
    n = np.random.standard_normal
    s = mx_kscale(K)[:, None]
    p_tab = pack_weight(n((K, T)) * s, "e4m3")
    return {
        "tab_words": p_tab[0],
        "tab_scales": p_tab[1],
        "wg": (n((K, N)) / np.sqrt(K) / s).astype(np.float32),
        "wh": (n((K, N)) / np.sqrt(K) / s).astype(np.float32),
        "bg": (0.3 * n(N) - 1.0).astype(np.float32),
        "rT": (n((N, T))).astype(np.float32),
        "offs": striped(np.random.permutation(T)[:J]),
    }


def reference(tab_words, tab_scales, wg, wh, bg, rT, offs):
    idx = unstriped(offs)
    tab_ = unpack_weight(tab_words, tab_scales, "e4m3")[:, idx]
    wg_ = mxq(f64(wg), 0, "e4m3")
    wh_ = mxq(f64(wh), 0, "e4m3")
    ga = wg_.T @ tab_
    gate = sigm(ga + f64(bg)[:, None])
    ha = wh_.T @ tab_
    out_0 = f64(rT)[:, idx] + gate * (np.maximum(ha, 0.0) - f64(rT)[:, idx])
    return (out_0,) + planes(out_0)

@@ -1,0 +1,182 @@
+from contextlib import ExitStack
+
+import concourse.mybir as mybir
+
+K, N, T, J = 512, 512, 2048, 1024
+FLOPS = 2 * 2 * K * N * J
+
+F32 = mybir.dt.float32
+BF16 = mybir.dt.bfloat16
+I32 = mybir.dt.int32
+U32 = mybir.dt.uint32
+U16 = mybir.dt.uint16
+U8 = mybir.dt.uint8
+FP8X4 = mybir.dt.float8_e4m3fn_x4
+ALU = mybir.AluOpType
+ACT = mybir.ActivationFunctionType
+
+P = 128
+PACK = 4
+HALF = 512
+UNITS = [(0, 0), (0, 1), (1, 0), (2, 0), (3, 0), (1, 1), (2, 1), (3, 1)]
+PIECES = {0: [(0, 512)], 1: [(0, 256), (256, 128), (384, 128)]}
+
+
+def tile_list_hwayt_reluP_kernel(
+    tc, tab_words, tab_scales, wg, wh, bg, rT, offs, out_0, out_1, out_2
+):
+    nc = tc.nc
+    with ExitStack() as ctx:
+        keep = ctx.enter_context(tc.tile_pool(name="keep", bufs=1))
+        ring = ctx.enter_context(tc.tile_pool(name="ring", bufs=3))
+        psum = ctx.enter_context(tc.psum_pool(name="psum", bufs=3))
+
+        offsets = keep.tile([P, J // 16], U16, name="offsets")
+        nc.sync.dma_start(offsets[:], offs)
+
+        plane = keep.tile([P, T], U8, name="plane", align_bytes=64)
+        nc.vector.memset(plane[:].bitcast(I32), 0)
+        for q in range(4):
+            nc.scalar.dma_start(
+                plane[32 * q : 32 * q + 4, :].bitcast(I32),
+                tab_scales[0, 4 * q : 4 * q + 4, :].bitcast(I32),
+            )
+
+        warm_in = keep.tile([P, 1], F32, name="warm_in")
+        warm_out = keep.tile([P, 1], F32, name="warm_out")
+        nc.gpsimd.memset(warm_in[:], 0.0)
+        nc.scalar.activation(warm_out[:], warm_in[:], ACT.Sigmoid)
+
+        def load_w(w, name):
+            raw = keep.tile([P, PACK, N], F32, name=name + "_raw")
+            nc.sync.dma_start(raw[:], w.rearrange("(p i) n -> p i n", i=PACK))
+            return raw
+
+        r_rows = rT.rearrange("(p t) c -> p t c", t=PACK)
+
+        def load_r(t):
+            r = keep.tile([P, T], F32, name="r%d" % t)
+            nc.sync.dma_start(r[:], r_rows[:, t, :])
+            return r
+
+        wg_raw = load_w(wg, "wg")
+        words = keep.tile([P, T], U32, name="words", align_bytes=64)
+        nc.sync.dma_start(words[:].bitcast(I32), tab_words[0].rearrange("p c i -> p (c i)").bitcast(I32))
+        r_sb = [load_r(0)]
+        bias = keep.tile([P, PACK], F32, name="bias")
+        nc.sync.dma_start(bias[:], bg.rearrange("(p t) -> p t", t=PACK))
+        wh_raw = load_w(wh, "wh")
+        for t in range(1, PACK):
+            r_sb.append(load_r(t))
+
+        neg_bias = keep.tile([P, PACK], F32, name="neg_bias")
+        nc.gpsimd.tensor_scalar(neg_bias[:], bias[:], -1.0, 0.0, ALU.mult, ALU.add)
+
+        def round_w(raw, name):
+            grouped = keep.tile([P, PACK * N], BF16, name=name + "_bf", align_bytes=64)
+            nc.scalar.copy(
+                grouped[:].rearrange("p (t m i) -> p m i t", t=PACK, i=PACK),
+                raw[:].rearrange("p i (m t) -> p m i t", t=PACK),
+            )
+            return grouped
+
+        def quantize_w(grouped, name):
+            codes = keep.tile([P, N], U32, name=name + "_codes", align_bytes=64)
+            scales = keep.tile([P, N], U8, name=name + "_scales", align_bytes=64)
+            nc.vector.quantize_mx(out=codes[:].bitcast(FP8X4), scales=scales[:], in_=grouped[:])
+            return codes, scales
+
+        def list_cols(j0, width):
+            return offsets[:, j0 // 16 : (j0 + width) // 16]
+
+        def gather_table(half):
+            scales = keep.tile([P, HALF], U8, name="v_scales%d" % half, align_bytes=64)
+            nc.vector.tensor_copy(scales[:], plane[:].indirect(list_cols(half * HALF, HALF)))
+            codes = keep.tile([P, HALF], U32, name="v_codes%d" % half, align_bytes=64)
+            nc.vector.tensor_copy(codes[:], words[:].indirect(list_cols(half * HALF, HALF)))
+            return codes, scales
+
+        wg_bf = round_w(wg_raw, "wg")
+        v = [gather_table(0)]
+        wg_q = quantize_w(wg_bf, "wg")
+        v.append(gather_table(1))
+        wh_bf = round_w(wh_raw, "wh")
+        wh_q = quantize_w(wh_bf, "wh")
+
+        def product(w_q, t, half, name):
+            acc = psum.tile([P, HALF], F32, name=name)
+            cols = slice(t * P, (t + 1) * P)
+            nc.tensor.matmul_mx(
+                out=acc[:],
+                lhsT=w_q[0][:, cols].bitcast(FP8X4),
+                lhsT_scale=w_q[1][:, cols],
+                rhs=v[half][0][:].bitcast(FP8X4),
+                rhs_scale=v[half][1][:],
+                start=True,
+                stop=True,
+            )
+            return acc
+
+        y = [keep.tile([P, PACK, HALF], F32, name="y%d" % h) for h in range(2)]
+        y_codes = keep.tile([P, J], U32, name="y_codes", align_bytes=64)
+        y_scales = keep.tile([P, J], U8, name="y_scales", align_bytes=64)
+        out_rows = out_0.rearrange("(p t) j -> p t j", t=PACK)
+        out_words = out_1[0].rearrange("p j i -> p (j i)").bitcast(I32)
+
+        def terms(t, half):
+            ga = product(wg_q, t, half, "ga")
+            carry = ring.tile([P, HALF], F32, name="carry")
+            nc.scalar.activation(carry[:], ga[:], ACT.Sigmoid, bias=neg_bias[:, t : t + 1], scale=-1.0)
+            gate = ring.tile([P, HALF], F32, name="gate")
+            nc.scalar.activation(gate[:], ga[:], ACT.Sigmoid, bias=bias[:, t : t + 1])
+            ha = product(wh_q, t, half, "ha")
+            kept = ring.tile([P, HALF], F32, name="kept")
+            pieces = PIECES[half] if t == PACK - 1 else [(0, HALF)]
+            made = ring.tile([P, HALF], F32, name="made")
+            first = True
+            for c0, w in pieces:
+                nc.vector.tensor_tensor(
+                    kept[:, c0 : c0 + w],
+                    r_sb[t][:].indirect(list_cols(half * HALF + c0, w)),
+                    carry[:, c0 : c0 + w],
+                    ALU.mult,
+                )
+                if first:
+                    nc.vector.scalar_tensor_tensor(made[:], ha[:], 0.0, gate[:], ALU.max, ALU.mult)
+                    first = False
+            return kept, made
+
+        def finish(t, half, kept, made):
+            pieces = PIECES[half] if t == PACK - 1 else [(0, HALF)]
+            for c0, w in pieces:
+                cols = slice(c0, c0 + w)
+                j0 = half * HALF + c0
+                nc.vector.tensor_tensor(y[half][:, t, cols], kept[:, cols], made[:, cols], ALU.add)
+                nc.sync.dma_start(out_rows[:, t, j0 : j0 + w], y[half][:, t, cols])
+                if t == PACK - 1:
+                    rounded = keep.tile([P, PACK * w], BF16, name="rounded%d" % j0, align_bytes=64)
+                    nc.scalar.copy(
+                        rounded[:].rearrange("p (c e t) -> p c t e", e=4, t=PACK),
+                        y[half][:, :, cols].rearrange("p t (c e) -> p c t e", e=4),
+                    )
+                    nc.vector.quantize_mx(
+                        out=y_codes[:, j0 : j0 + w].bitcast(FP8X4),
+                        scales=y_scales[:, j0 : j0 + w],
+                        in_=rounded[:],
+                    )
+                    nc.sync.dma_start(out_words[:, j0 : j0 + w], y_codes[:, j0 : j0 + w].bitcast(I32))
+
+        waiting = None
+        for t, half in UNITS:
+            kept, made = terms(t, half)
+            if waiting is not None:
+                finish(*waiting)
+            waiting = (t, half, kept, made)
+        finish(*waiting)
+
+        for q in range(4):
+            queue = nc.scalar if q % 2 else nc.sync
+            queue.dma_start(
+                out_2[0, 4 * q : 4 * q + 4, :].bitcast(I32),
+                y_scales[32 * q : 32 * q + 4, :].bitcast(I32),
+            )

@@ -29,23 +29,7 @@ def tile_list_hwayt_reluP_kernel(
     with ExitStack() as ctx:
         keep = ctx.enter_context(tc.tile_pool(name="keep", bufs=1))
         ring = ctx.enter_context(tc.tile_pool(name="ring", bufs=3))
-        psum = ctx.enter_context(tc.psum_pool(name="psum", bufs=3))
-
-        offsets = keep.tile([P, J // 16], U16, name="offsets")
-        nc.sync.dma_start(offsets[:], offs)
-
-        plane = keep.tile([P, T], U8, name="plane", align_bytes=64)
-        nc.vector.memset(plane[:].bitcast(I32), 0)
-        for q in range(4):
-            nc.scalar.dma_start(
-                plane[32 * q : 32 * q + 4, :].bitcast(I32),
-                tab_scales[0, 4 * q : 4 * q + 4, :].bitcast(I32),
-            )
-
-        warm_in = keep.tile([P, 1], F32, name="warm_in")
-        warm_out = keep.tile([P, 1], F32, name="warm_out")
-        nc.gpsimd.memset(warm_in[:], 0.0)
-        nc.scalar.activation(warm_out[:], warm_in[:], ACT.Sigmoid)
+        psum = ctx.enter_context(tc.psum_pool(name="psum", bufs=2))
 
         def load_w(w, name):
             raw = keep.tile([P, PACK, N], F32, name=name + "_raw")
@@ -60,58 +44,78 @@ def tile_list_hwayt_reluP_kernel(
             return r
 
         wg_raw = load_w(wg, "wg")
+        scale_rows = keep.tile([P, T // 4], I32, name="scale_rows")
+        for q in range(4):
+            nc.sync.dma_start(
+                scale_rows[32 * q : 32 * q + 4, :],
+                tab_scales[0, 4 * q : 4 * q + 4, :].bitcast(I32),
+            )
+        offsets = keep.tile([P, J // 16], U16, name="offsets")
+        nc.sync.dma_start(offsets[:], offs)
+        wh_raw = load_w(wh, "wh")
         words = keep.tile([P, T], U32, name="words", align_bytes=64)
         nc.sync.dma_start(words[:].bitcast(I32), tab_words[0].rearrange("p c i -> p (c i)").bitcast(I32))
-        r_sb = [load_r(0)]
+        r_sb = [load_r(t) for t in range(PACK)]
+
         bias = keep.tile([P, PACK], F32, name="bias")
-        nc.sync.dma_start(bias[:], bg.rearrange("(p t) -> p t", t=PACK))
-        wh_raw = load_w(wh, "wh")
-        for t in range(1, PACK):
-            r_sb.append(load_r(t))
+        nc.gpsimd.dma_start(bias[:], bg.rearrange("(p t) -> p t", t=PACK))
+
+        warm_in = keep.tile([P, 1], F32, name="warm_in")
+        warm_out = keep.tile([P, 1], F32, name="warm_out")
+        nc.vector.memset(warm_in[:], 0.0)
+        nc.scalar.activation(warm_out[:], warm_in[:], ACT.Sigmoid)
+
+        plane = keep.tile([P, T], U8, name="plane", align_bytes=64)
+        nc.vector.memset(plane[:].bitcast(I32), 0)
+        for q in range(4):
+            live = slice(32 * q, 32 * q + 4)
+            nc.vector.tensor_copy(plane[live, :].bitcast(I32), scale_rows[live, :])
 
         neg_bias = keep.tile([P, PACK], F32, name="neg_bias")
         nc.gpsimd.tensor_scalar(neg_bias[:], bias[:], -1.0, 0.0, ALU.mult, ALU.add)
 
-        def round_w(raw, name):
-            grouped = keep.tile([P, PACK * N], BF16, name=name + "_bf", align_bytes=64)
+        def round_w(raw, pair, name):
+            grouped = keep.tile([P, 2 * N], BF16, name="%s_bf%d" % (name, pair), align_bytes=64)
             nc.scalar.copy(
-                grouped[:].rearrange("p (t m i) -> p m i t", t=PACK, i=PACK),
-                raw[:].rearrange("p i (m t) -> p m i t", t=PACK),
+                grouped[:].rearrange("p (t m i) -> p m i t", t=2, i=PACK),
+                raw[:].rearrange("p i (m t) -> p m i t", t=PACK)[:, :, :, 2 * pair : 2 * pair + 2],
             )
             return grouped
 
-        def quantize_w(grouped, name):
-            codes = keep.tile([P, N], U32, name=name + "_codes", align_bytes=64)
-            scales = keep.tile([P, N], U8, name=name + "_scales", align_bytes=64)
+        def quantize_w(grouped, pair, name):
+            codes = keep.tile([P, 2 * P], U32, name="%s_codes%d" % (name, pair), align_bytes=64)
+            scales = keep.tile([P, 2 * P], U8, name="%s_scales%d" % (name, pair), align_bytes=64)
             nc.vector.quantize_mx(out=codes[:].bitcast(FP8X4), scales=scales[:], in_=grouped[:])
             return codes, scales
 
         def list_cols(j0, width):
             return offsets[:, j0 // 16 : (j0 + width) // 16]
 
-        def gather_table(half):
+        def gather_scales(half):
             scales = keep.tile([P, HALF], U8, name="v_scales%d" % half, align_bytes=64)
             nc.vector.tensor_copy(scales[:], plane[:].indirect(list_cols(half * HALF, HALF)))
+            return scales
+
+        def gather_codes(half):
             codes = keep.tile([P, HALF], U32, name="v_codes%d" % half, align_bytes=64)
             nc.vector.tensor_copy(codes[:], words[:].indirect(list_cols(half * HALF, HALF)))
-            return codes, scales
+            return codes
 
-        wg_bf = round_w(wg_raw, "wg")
-        v = [gather_table(0)]
-        wg_q = quantize_w(wg_bf, "wg")
-        v.append(gather_table(1))
-        wh_bf = round_w(wh_raw, "wh")
-        wh_q = quantize_w(wh_bf, "wh")
+        v_scales = [gather_scales(half) for half in range(2)]
+        wg_q = [quantize_w(round_w(wg_raw, pair, "wg"), pair, "wg") for pair in range(2)]
+        wh_q = [quantize_w(round_w(wh_raw, 0, "wh"), 0, "wh")]
+        v_codes = [gather_codes(half) for half in range(2)]
+        wh_q.append(quantize_w(round_w(wh_raw, 1, "wh"), 1, "wh"))
 
-        def product(w_q, t, half, name):
-            acc = psum.tile([P, HALF], F32, name=name)
-            cols = slice(t * P, (t + 1) * P)
+        def product(w_q, t, half, name, bufs):
+            acc = psum.tile([P, HALF], F32, name=name, bufs=bufs)
+            cols = slice(t % 2 * P, (t % 2 + 1) * P)
             nc.tensor.matmul_mx(
                 out=acc[:],
-                lhsT=w_q[0][:, cols].bitcast(FP8X4),
-                lhsT_scale=w_q[1][:, cols],
-                rhs=v[half][0][:].bitcast(FP8X4),
-                rhs_scale=v[half][1][:],
+                lhsT=w_q[t // 2][0][:, cols].bitcast(FP8X4),
+                lhsT_scale=w_q[t // 2][1][:, cols],
+                rhs=v_codes[half][:].bitcast(FP8X4),
+                rhs_scale=v_scales[half][:],
                 start=True,
                 stop=True,
             )
@@ -124,12 +128,12 @@ def tile_list_hwayt_reluP_kernel(
         out_words = out_1[0].rearrange("p j i -> p (j i)").bitcast(I32)
 
         def terms(t, half):
-            ga = product(wg_q, t, half, "ga")
-            carry = ring.tile([P, HALF], F32, name="carry")
+            ga = product(wg_q, t, half, "ga", 2)
+            carry = ring.tile([P, HALF], F32, name="carry", bufs=8)
             nc.scalar.activation(carry[:], ga[:], ACT.Sigmoid, bias=neg_bias[:, t : t + 1], scale=-1.0)
-            gate = ring.tile([P, HALF], F32, name="gate")
+            gate = ring.tile([P, HALF], F32, name="gate", bufs=8)
             nc.scalar.activation(gate[:], ga[:], ACT.Sigmoid, bias=bias[:, t : t + 1])
-            ha = product(wh_q, t, half, "ha")
+            ha = product(wh_q, t, half, "ha", 6)
             kept = ring.tile([P, HALF], F32, name="kept")
             pieces = PIECES[half] if t == PACK - 1 else [(0, HALF)]
             made = ring.tile([P, HALF], F32, name="made")
@@ -153,21 +157,27 @@ def tile_list_hwayt_reluP_kernel(
                 j0 = half * HALF + c0
                 nc.vector.tensor_tensor(y[half][:, t, cols], kept[:, cols], made[:, cols], ALU.add)
                 nc.sync.dma_start(out_rows[:, t, j0 : j0 + w], y[half][:, t, cols])
-                if t == PACK - 1:
-                    rounded = keep.tile([P, PACK * w], BF16, name="rounded%d" % j0, align_bytes=64)
-                    nc.scalar.copy(
-                        rounded[:].rearrange("p (c e t) -> p c t e", e=4, t=PACK),
-                        y[half][:, :, cols].rearrange("p t (c e) -> p c t e", e=4),
-                    )
-                    nc.vector.quantize_mx(
-                        out=y_codes[:, j0 : j0 + w].bitcast(FP8X4),
-                        scales=y_scales[:, j0 : j0 + w],
-                        in_=rounded[:],
-                    )
-                    nc.sync.dma_start(out_words[:, j0 : j0 + w], y_codes[:, j0 : j0 + w].bitcast(I32))
+                if t == PACK - 1 and half == 1:
+                    planes(half, c0, w)
+
+        def planes(half, c0, w):
+            j0 = half * HALF + c0
+            rounded = keep.tile([P, PACK * w], BF16, name="rounded%d" % j0, align_bytes=64)
+            nc.scalar.copy(
+                rounded[:].rearrange("p (c e t) -> p c t e", e=4, t=PACK),
+                y[half][:, :, c0 : c0 + w].rearrange("p t (c e) -> p c t e", e=4),
+            )
+            nc.vector.quantize_mx(
+                out=y_codes[:, j0 : j0 + w].bitcast(FP8X4),
+                scales=y_scales[:, j0 : j0 + w],
+                in_=rounded[:],
+            )
+            nc.sync.dma_start(out_words[:, j0 : j0 + w], y_codes[:, j0 : j0 + w].bitcast(I32))
 
         waiting = None
         for t, half in UNITS:
+            if (t, half) == (PACK - 1, 1):
+                planes(0, 0, HALF)
             kept, made = terms(t, half)
             if waiting is not None:
                 finish(*waiting)

@@ -1,6 +1,7 @@
 from contextlib import ExitStack
 
 import concourse.mybir as mybir
+from concourse.masks import make_identity
 
 K, N, T, J = 512, 512, 2048, 1024
 FLOPS = 2 * 2 * K * N * J
@@ -19,7 +20,8 @@ P = 128
 PACK = 4
 HALF = 512
 UNITS = [(0, 0), (0, 1), (1, 0), (2, 0), (3, 0), (1, 1), (2, 1), (3, 1)]
-PIECES = {0: [(0, 512)], 1: [(0, 256), (256, 128), (384, 128)]}
+ON_TENSOR = 4
+QUARTER = HALF // 2
 
 
 def tile_list_hwayt_reluP_kernel(
@@ -28,7 +30,7 @@ def tile_list_hwayt_reluP_kernel(
     nc = tc.nc
     with ExitStack() as ctx:
         keep = ctx.enter_context(tc.tile_pool(name="keep", bufs=1))
-        ring = ctx.enter_context(tc.tile_pool(name="ring", bufs=3))
+        ring = ctx.enter_context(tc.tile_pool(name="ring", bufs=8))
         psum = ctx.enter_context(tc.psum_pool(name="psum", bufs=2))
 
         def load_w(w, name):
@@ -43,13 +45,13 @@ def tile_list_hwayt_reluP_kernel(
             nc.sync.dma_start(r[:], r_rows[:, t, :])
             return r
 
-        wg_raw = load_w(wg, "wg")
         scale_rows = keep.tile([P, T // 4], I32, name="scale_rows")
         for q in range(4):
             nc.sync.dma_start(
                 scale_rows[32 * q : 32 * q + 4, :],
                 tab_scales[0, 4 * q : 4 * q + 4, :].bitcast(I32),
             )
+        wg_raw = load_w(wg, "wg")
         offsets = keep.tile([P, J // 16], U16, name="offsets")
         nc.sync.dma_start(offsets[:], offs)
         wh_raw = load_w(wh, "wh")
@@ -71,6 +73,8 @@ def tile_list_hwayt_reluP_kernel(
             live = slice(32 * q, 32 * q + 4)
             nc.vector.tensor_copy(plane[live, :].bitcast(I32), scale_rows[live, :])
 
+        ident = keep.tile([P, P], F32, name="ident")
+        make_identity(nc, ident[:])
         neg_bias = keep.tile([P, PACK], F32, name="neg_bias")
         nc.gpsimd.tensor_scalar(neg_bias[:], bias[:], -1.0, 0.0, ALU.mult, ALU.add)
 
@@ -127,62 +131,122 @@ def tile_list_hwayt_reluP_kernel(
         out_rows = out_0.rearrange("(p t) j -> p t j", t=PACK)
         out_words = out_1[0].rearrange("p j i -> p (j i)").bitcast(I32)
 
-        def terms(t, half):
+        carry, gate, ha, kept, made, turned = {}, {}, {}, {}, {}, {}
+
+        def gates(u):
+            t, half = u
             ga = product(wg_q, t, half, "ga", 2)
-            carry = ring.tile([P, HALF], F32, name="carry", bufs=8)
-            nc.scalar.activation(carry[:], ga[:], ACT.Sigmoid, bias=neg_bias[:, t : t + 1], scale=-1.0)
-            gate = ring.tile([P, HALF], F32, name="gate", bufs=8)
-            nc.scalar.activation(gate[:], ga[:], ACT.Sigmoid, bias=bias[:, t : t + 1])
-            ha = product(wh_q, t, half, "ha", 6)
-            kept = ring.tile([P, HALF], F32, name="kept")
-            pieces = PIECES[half] if t == PACK - 1 else [(0, HALF)]
-            made = ring.tile([P, HALF], F32, name="made")
-            first = True
-            for c0, w in pieces:
-                nc.vector.tensor_tensor(
-                    kept[:, c0 : c0 + w],
-                    r_sb[t][:].indirect(list_cols(half * HALF + c0, w)),
-                    carry[:, c0 : c0 + w],
-                    ALU.mult,
-                )
-                if first:
-                    nc.vector.scalar_tensor_tensor(made[:], ha[:], 0.0, gate[:], ALU.max, ALU.mult)
-                    first = False
-            return kept, made
+            carry[u] = ring.tile([P, HALF], F32, name="carry")
+            nc.scalar.activation(carry[u][:], ga[:], ACT.Sigmoid, bias=neg_bias[:, t : t + 1], scale=-1.0)
+            gate[u] = ring.tile([P, HALF], F32, name="gate")
+            nc.scalar.activation(gate[u][:], ga[:], ACT.Sigmoid, bias=bias[:, t : t + 1])
+            ha[u] = product(wh_q, t, half, "ha", 3)
+            kept[u] = ring.tile([P, HALF], F32, name="kept")
+            made[u] = ring.tile([P, HALF], F32, name="made")
 
-        def finish(t, half, kept, made):
-            pieces = PIECES[half] if t == PACK - 1 else [(0, HALF)]
-            for c0, w in pieces:
-                cols = slice(c0, c0 + w)
-                j0 = half * HALF + c0
-                nc.vector.tensor_tensor(y[half][:, t, cols], kept[:, cols], made[:, cols], ALU.add)
-                nc.sync.dma_start(out_rows[:, t, j0 : j0 + w], y[half][:, t, cols])
-                if t == PACK - 1 and half == 1:
-                    planes(half, c0, w)
+        def keep_part(u, c0, w):
+            t, half = u
+            nc.vector.tensor_tensor(
+                kept[u][:, c0 : c0 + w],
+                r_sb[t][:].indirect(list_cols(half * HALF + c0, w)),
+                carry[u][:, c0 : c0 + w],
+                ALU.mult,
+            )
 
-        def planes(half, c0, w):
-            j0 = half * HALF + c0
-            rounded = keep.tile([P, PACK * w], BF16, name="rounded%d" % j0, align_bytes=64)
-            nc.scalar.copy(
+        def make_part(u):
+            nc.vector.scalar_tensor_tensor(made[u][:], ha[u][:], 0.0, gate[u][:], ALU.max, ALU.mult)
+
+        def store_y(u):
+            t, half = u
+            nc.sync.dma_start(out_rows[:, t, half * HALF : (half + 1) * HALF], y[half][:, t, :])
+
+        def add_on_vector(u, c0, w):
+            t, half = u
+            cols = slice(c0, c0 + w)
+            nc.vector.tensor_tensor(y[half][:, t, cols], kept[u][:, cols], made[u][:, cols], ALU.add)
+
+        def add_on_tensor(u):
+            bank = psum.tile([P, HALF], F32, name="sum_t", bufs=2)
+            for c0 in range(0, HALF, P):
+                cols = slice(c0, c0 + P)
+                nc.tensor.matmul(bank[:, cols], made[u][:, cols], ident[:], start=True, stop=False, is_transpose=True)
+                nc.tensor.matmul(bank[:, cols], kept[u][:, cols], ident[:], start=False, stop=True, is_transpose=True)
+            turned[u] = ring.tile([P, HALF], F32, name="turned", bufs=2)
+            nc.scalar.copy(turned[u][:], bank[:])
+
+        def turn_back(u):
+            t, half = u
+            bank = psum.tile([P, HALF], F32, name="back", bufs=1)
+            for c0 in range(0, HALF, P):
+                cols = slice(c0, c0 + P)
+                nc.tensor.transpose(bank[:, cols], turned[u][:, cols], ident[:])
+            nc.scalar.copy(y[half][:, t, :], bank[:])
+            store_y(u)
+
+        def round_y(copy, half, c0, w):
+            rounded = keep.tile([P, PACK * w], BF16, name="rounded%d" % (half * HALF + c0), align_bytes=64)
+            copy(
                 rounded[:].rearrange("p (c e t) -> p c t e", e=4, t=PACK),
                 y[half][:, :, c0 : c0 + w].rearrange("p t (c e) -> p c t e", e=4),
             )
+            return rounded
+
+        def quantize_y(rounded, half, c0, w):
+            j0 = half * HALF + c0
             nc.vector.quantize_mx(
                 out=y_codes[:, j0 : j0 + w].bitcast(FP8X4),
                 scales=y_scales[:, j0 : j0 + w],
                 in_=rounded[:],
             )
+
+        def store_codes(j0, w):
             nc.sync.dma_start(out_words[:, j0 : j0 + w], y_codes[:, j0 : j0 + w].bitcast(I32))
 
-        waiting = None
-        for t, half in UNITS:
-            if (t, half) == (PACK - 1, 1):
-                planes(0, 0, HALF)
-            kept, made = terms(t, half)
-            if waiting is not None:
-                finish(*waiting)
-            waiting = (t, half, kept, made)
-        finish(*waiting)
+        whole = UNITS[:-2]
+        for i, u in enumerate(whole):
+            gates(u)
+            keep_part(u, 0, HALF)
+            make_part(u)
+            if ON_TENSOR < i:
+                add_on_vector(UNITS[i - 1], 0, HALF)
+                store_y(UNITS[i - 1])
+            if 0 <= i - 4 < ON_TENSOR:
+                turn_back(UNITS[i - 4])
+            if 0 <= i - 3 < ON_TENSOR:
+                add_on_tensor(UNITS[i - 3])
+
+        u2, u3 = UNITS[-2:]
+        gates(u2)
+        turn_back(UNITS[2])
+        add_on_tensor(UNITS[3])
+        gates(u3)
+        turn_back(UNITS[3])
+        first_half = round_y(nc.scalar.copy, 0, 0, HALF)
+        keep_part(u2, 0, QUARTER)
+        make_part(u2)
+        add_on_vector(whole[-1], 0, HALF)
+        store_y(whole[-1])
+        keep_part(u3, 0, QUARTER)
+        make_part(u3)
+        add_on_vector(u2, 0, QUARTER)
+        add_on_vector(u3, 0, QUARTER)
+        third = round_y(nc.scalar.copy, 1, 0, QUARTER)
+        keep_part(u2, QUARTER, QUARTER)
+        quantize_y(first_half, 0, 0, HALF)
+        store_codes(0, HALF)
+        keep_part(u3, QUARTER, QUARTER)
+        add_on_vector(u2, QUARTER, QUARTER)
+        store_y(u2)
+        add_on_vector(u3, QUARTER, QUARTER)
+        store_y(u3)
+        eighth = QUARTER // 2
+        by_scalar = round_y(nc.scalar.copy, 1, QUARTER, eighth)
+        quantize_y(third, 1, 0, QUARTER)
+        store_codes(HALF, QUARTER)
+        by_vector = round_y(nc.vector.tensor_copy, 1, QUARTER + eighth, eighth)
+        quantize_y(by_scalar, 1, QUARTER, eighth)
+        quantize_y(by_vector, 1, QUARTER + eighth, eighth)
+        store_codes(HALF + QUARTER, QUARTER)
 
         for q in range(4):
             queue = nc.scalar if q % 2 else nc.sync

@@ -19,8 +19,6 @@ ACT = mybir.ActivationFunctionType
 P = 128
 PACK = 4
 HALF = 512
-UNITS = [(0, 0), (0, 1), (1, 0), (2, 0), (3, 0), (1, 1), (2, 1), (3, 1)]
-ON_TENSOR = 4
 QUARTER = HALF // 2
 
 
@@ -51,16 +49,16 @@ def tile_list_hwayt_reluP_kernel(
                 scale_rows[32 * q : 32 * q + 4, :],
                 tab_scales[0, 4 * q : 4 * q + 4, :].bitcast(I32),
             )
-        wg_raw = load_w(wg, "wg")
         offsets = keep.tile([P, J // 16], U16, name="offsets")
         nc.sync.dma_start(offsets[:], offs)
-        wh_raw = load_w(wh, "wh")
         words = keep.tile([P, T], U32, name="words", align_bytes=64)
         nc.sync.dma_start(words[:].bitcast(I32), tab_words[0].rearrange("p c i -> p (c i)").bitcast(I32))
+        wg_raw = load_w(wg, "wg")
+        wh_raw = load_w(wh, "wh")
         r_sb = [load_r(t) for t in range(PACK)]
 
         bias = keep.tile([P, PACK], F32, name="bias")
-        nc.gpsimd.dma_start(bias[:], bg.rearrange("(p t) -> p t", t=PACK))
+        nc.scalar.dma_start(bias[:], bg.rearrange("(p t) -> p t", t=PACK))
 
         warm_in = keep.tile([P, 1], F32, name="warm_in")
         warm_out = keep.tile([P, 1], F32, name="warm_out")
@@ -78,9 +76,9 @@ def tile_list_hwayt_reluP_kernel(
         neg_bias = keep.tile([P, PACK], F32, name="neg_bias")
         nc.gpsimd.tensor_scalar(neg_bias[:], bias[:], -1.0, 0.0, ALU.mult, ALU.add)
 
-        def round_w(raw, pair, name):
+        def round_w(copy, raw, pair, name):
             grouped = keep.tile([P, 2 * N], BF16, name="%s_bf%d" % (name, pair), align_bytes=64)
-            nc.scalar.copy(
+            copy(
                 grouped[:].rearrange("p (t m i) -> p m i t", t=2, i=PACK),
                 raw[:].rearrange("p i (m t) -> p m i t", t=PACK)[:, :, :, 2 * pair : 2 * pair + 2],
             )
@@ -106,10 +104,11 @@ def tile_list_hwayt_reluP_kernel(
             return codes
 
         v_scales = [gather_scales(half) for half in range(2)]
-        wg_q = [quantize_w(round_w(wg_raw, pair, "wg"), pair, "wg") for pair in range(2)]
-        wh_q = [quantize_w(round_w(wh_raw, 0, "wh"), 0, "wh")]
         v_codes = [gather_codes(half) for half in range(2)]
-        wh_q.append(quantize_w(round_w(wh_raw, 1, "wh"), 1, "wh"))
+        wg_bf = [round_w(nc.scalar.copy, wg_raw, pair, "wg") for pair in range(2)]
+        wg_q = [quantize_w(wg_bf[pair], pair, "wg") for pair in range(2)]
+        wh_bf = [round_w(nc.vector.tensor_copy, wh_raw, pair, "wh") for pair in range(2)]
+        wh_q = [quantize_w(wh_bf[pair], pair, "wh") for pair in range(2)]
 
         def product(w_q, t, half, name, bufs):
             acc = psum.tile([P, HALF], F32, name=name, bufs=bufs)
@@ -141,8 +140,8 @@ def tile_list_hwayt_reluP_kernel(
             gate[u] = ring.tile([P, HALF], F32, name="gate")
             nc.scalar.activation(gate[u][:], ga[:], ACT.Sigmoid, bias=bias[:, t : t + 1])
             ha[u] = product(wh_q, t, half, "ha", 3)
-            kept[u] = ring.tile([P, HALF], F32, name="kept")
-            made[u] = ring.tile([P, HALF], F32, name="made")
+            kept[u] = carry[(3, 0)] if u == (2, 1) else ring.tile([P, HALF], F32, name="kept")
+            made[u] = carry[u] if t < 2 else ring.tile([P, HALF], F32, name="made")
 
         def keep_part(u, c0, w):
             t, half = u
@@ -165,22 +164,22 @@ def tile_list_hwayt_reluP_kernel(
             cols = slice(c0, c0 + w)
             nc.vector.tensor_tensor(y[half][:, t, cols], kept[u][:, cols], made[u][:, cols], ALU.add)
 
-        def add_on_tensor(u):
-            bank = psum.tile([P, HALF], F32, name="sum_t", bufs=2)
-            for c0 in range(0, HALF, P):
+        def add_on_tensor(u, first):
+            bank = psum.tile([P, HALF], F32, name="turn", bufs=3)
+            for c0 in range(first, HALF, P):
                 cols = slice(c0, c0 + P)
                 nc.tensor.matmul(bank[:, cols], made[u][:, cols], ident[:], start=True, stop=False, is_transpose=True)
                 nc.tensor.matmul(bank[:, cols], kept[u][:, cols], ident[:], start=False, stop=True, is_transpose=True)
-            turned[u] = ring.tile([P, HALF], F32, name="turned", bufs=2)
-            nc.scalar.copy(turned[u][:], bank[:])
+            turned[u] = ring.tile([P, HALF], F32, name="turned", bufs=3)
+            nc.scalar.copy(turned[u][:, first:], bank[:, first:])
 
-        def turn_back(u):
+        def turn_back(u, first):
             t, half = u
-            bank = psum.tile([P, HALF], F32, name="back", bufs=1)
-            for c0 in range(0, HALF, P):
+            bank = psum.tile([P, HALF], F32, name="turn", bufs=3)
+            for c0 in range(first, HALF, P):
                 cols = slice(c0, c0 + P)
                 nc.tensor.transpose(bank[:, cols], turned[u][:, cols], ident[:])
-            nc.scalar.copy(y[half][:, t, :], bank[:])
+            nc.scalar.copy(y[half][:, t, first:], bank[:, first:])
             store_y(u)
 
         def round_y(copy, half, c0, w):
@@ -202,30 +201,36 @@ def tile_list_hwayt_reluP_kernel(
         def store_codes(j0, w):
             nc.sync.dma_start(out_words[:, j0 : j0 + w], y_codes[:, j0 : j0 + w].bitcast(I32))
 
-        whole = UNITS[:-2]
-        for i, u in enumerate(whole):
+        def terms(u):
             gates(u)
             keep_part(u, 0, HALF)
             make_part(u)
-            if ON_TENSOR < i:
-                add_on_vector(UNITS[i - 1], 0, HALF)
-                store_y(UNITS[i - 1])
-            if 0 <= i - 4 < ON_TENSOR:
-                turn_back(UNITS[i - 4])
-            if 0 <= i - 3 < ON_TENSOR:
-                add_on_tensor(UNITS[i - 3])
 
-        u2, u3 = UNITS[-2:]
+        for u in [(0, 0), (0, 1), (1, 0), (1, 1), (2, 0)]:
+            terms(u)
+        add_on_tensor((0, 0), 0)
+        add_on_tensor((0, 1), 0)
+        gates((3, 0))
+        keep_part((3, 0), 0, HALF)
+        add_on_vector((2, 0), 0, QUARTER)
+        make_part((3, 0))
+        turn_back((0, 0), 0)
+        turn_back((0, 1), 0)
+        add_on_tensor((1, 0), 0)
+
+        u2, u3 = (2, 1), (3, 1)
         gates(u2)
-        turn_back(UNITS[2])
-        add_on_tensor(UNITS[3])
+        add_on_tensor((1, 1), 0)
+        turn_back((1, 0), 0)
+        add_on_tensor((2, 0), QUARTER)
         gates(u3)
-        turn_back(UNITS[3])
-        first_half = round_y(nc.scalar.copy, 0, 0, HALF)
+        turn_back((2, 0), QUARTER)
+        turn_back((1, 1), 0)
         keep_part(u2, 0, QUARTER)
+        add_on_vector((3, 0), 0, HALF)
+        store_y((3, 0))
+        first_half = round_y(nc.scalar.copy, 0, 0, HALF)
         make_part(u2)
-        add_on_vector(whole[-1], 0, HALF)
-        store_y(whole[-1])
         keep_part(u3, 0, QUARTER)
         make_part(u3)
         add_on_vector(u2, 0, QUARTER)

from contextlib import ExitStack

import concourse.mybir as mybir
from concourse.masks import make_identity

K, N, T, J = 512, 512, 2048, 1024
FLOPS = 2 * 2 * K * N * J

F32 = mybir.dt.float32
BF16 = mybir.dt.bfloat16
I32 = mybir.dt.int32
U32 = mybir.dt.uint32
U16 = mybir.dt.uint16
U8 = mybir.dt.uint8
FP8X4 = mybir.dt.float8_e4m3fn_x4
ALU = mybir.AluOpType
ACT = mybir.ActivationFunctionType

P = 128
PACK = 4
HALF = 512
QUARTER = HALF // 2


def tile_list_hwayt_reluP_kernel(
    tc, tab_words, tab_scales, wg, wh, bg, rT, offs, out_0, out_1, out_2
):
    nc = tc.nc
    with ExitStack() as ctx:
        keep = ctx.enter_context(tc.tile_pool(name="keep", bufs=1))
        ring = ctx.enter_context(tc.tile_pool(name="ring", bufs=8))
        psum = ctx.enter_context(tc.psum_pool(name="psum", bufs=2))

        def load_w(w, name):
            raw = keep.tile([P, PACK, N], F32, name=name + "_raw")
            nc.sync.dma_start(raw[:], w.rearrange("(p i) n -> p i n", i=PACK))
            return raw

        r_rows = rT.rearrange("(p t) c -> p t c", t=PACK)

        def load_r(t):
            r = keep.tile([P, T], F32, name="r%d" % t)
            nc.sync.dma_start(r[:], r_rows[:, t, :])
            return r

        scale_rows = keep.tile([P, T // 4], I32, name="scale_rows")
        for q in range(4):
            nc.sync.dma_start(
                scale_rows[32 * q : 32 * q + 4, :],
                tab_scales[0, 4 * q : 4 * q + 4, :].bitcast(I32),
            )
        offsets = keep.tile([P, J // 16], U16, name="offsets")
        nc.sync.dma_start(offsets[:], offs)
        words = keep.tile([P, T], U32, name="words", align_bytes=64)
        nc.sync.dma_start(words[:].bitcast(I32), tab_words[0].rearrange("p c i -> p (c i)").bitcast(I32))
        wg_raw = load_w(wg, "wg")
        wh_raw = load_w(wh, "wh")
        r_sb = [load_r(t) for t in range(PACK)]

        bias = keep.tile([P, PACK], F32, name="bias")
        nc.scalar.dma_start(bias[:], bg.rearrange("(p t) -> p t", t=PACK))

        warm_in = keep.tile([P, 1], F32, name="warm_in")
        warm_out = keep.tile([P, 1], F32, name="warm_out")
        nc.vector.memset(warm_in[:], 0.0)
        nc.scalar.activation(warm_out[:], warm_in[:], ACT.Sigmoid)

        plane = keep.tile([P, T], U8, name="plane", align_bytes=64)
        nc.vector.memset(plane[:].bitcast(I32), 0)
        for q in range(4):
            live = slice(32 * q, 32 * q + 4)
            nc.vector.tensor_copy(plane[live, :].bitcast(I32), scale_rows[live, :])

        ident = keep.tile([P, P], F32, name="ident")
        make_identity(nc, ident[:])
        neg_bias = keep.tile([P, PACK], F32, name="neg_bias")
        nc.gpsimd.tensor_scalar(neg_bias[:], bias[:], -1.0, 0.0, ALU.mult, ALU.add)

        def round_w(copy, raw, pair, name):
            grouped = keep.tile([P, 2 * N], BF16, name="%s_bf%d" % (name, pair), align_bytes=64)
            copy(
                grouped[:].rearrange("p (t m i) -> p m i t", t=2, i=PACK),
                raw[:].rearrange("p i (m t) -> p m i t", t=PACK)[:, :, :, 2 * pair : 2 * pair + 2],
            )
            return grouped

        def quantize_w(grouped, pair, name):
            codes = keep.tile([P, 2 * P], U32, name="%s_codes%d" % (name, pair), align_bytes=64)
            scales = keep.tile([P, 2 * P], U8, name="%s_scales%d" % (name, pair), align_bytes=64)
            nc.vector.quantize_mx(out=codes[:].bitcast(FP8X4), scales=scales[:], in_=grouped[:])
            return codes, scales

        def list_cols(j0, width):
            return offsets[:, j0 // 16 : (j0 + width) // 16]

        def gather_scales(half):
            scales = keep.tile([P, HALF], U8, name="v_scales%d" % half, align_bytes=64)
            nc.vector.tensor_copy(scales[:], plane[:].indirect(list_cols(half * HALF, HALF)))
            return scales

        def gather_codes(half):
            codes = keep.tile([P, HALF], U32, name="v_codes%d" % half, align_bytes=64)
            nc.vector.tensor_copy(codes[:], words[:].indirect(list_cols(half * HALF, HALF)))
            return codes

        v_scales = [gather_scales(half) for half in range(2)]
        v_codes = [gather_codes(half) for half in range(2)]
        wg_bf = [round_w(nc.scalar.copy, wg_raw, pair, "wg") for pair in range(2)]
        wg_q = [quantize_w(wg_bf[pair], pair, "wg") for pair in range(2)]
        wh_bf = [round_w(nc.vector.tensor_copy, wh_raw, pair, "wh") for pair in range(2)]
        wh_q = [quantize_w(wh_bf[pair], pair, "wh") for pair in range(2)]

        def product(w_q, t, half, name, bufs):
            acc = psum.tile([P, HALF], F32, name=name, bufs=bufs)
            cols = slice(t % 2 * P, (t % 2 + 1) * P)
            nc.tensor.matmul_mx(
                out=acc[:],
                lhsT=w_q[t // 2][0][:, cols].bitcast(FP8X4),
                lhsT_scale=w_q[t // 2][1][:, cols],
                rhs=v_codes[half][:].bitcast(FP8X4),
                rhs_scale=v_scales[half][:],
                start=True,
                stop=True,
            )
            return acc

        y = [keep.tile([P, PACK, HALF], F32, name="y%d" % h) for h in range(2)]
        y_codes = keep.tile([P, J], U32, name="y_codes", align_bytes=64)
        y_scales = keep.tile([P, J], U8, name="y_scales", align_bytes=64)
        out_rows = out_0.rearrange("(p t) j -> p t j", t=PACK)
        out_words = out_1[0].rearrange("p j i -> p (j i)").bitcast(I32)

        carry, gate, ha, kept, made, turned = {}, {}, {}, {}, {}, {}

        def gates(u):
            t, half = u
            ga = product(wg_q, t, half, "ga", 2)
            carry[u] = ring.tile([P, HALF], F32, name="carry")
            nc.scalar.activation(carry[u][:], ga[:], ACT.Sigmoid, bias=neg_bias[:, t : t + 1], scale=-1.0)
            gate[u] = ring.tile([P, HALF], F32, name="gate")
            nc.scalar.activation(gate[u][:], ga[:], ACT.Sigmoid, bias=bias[:, t : t + 1])
            ha[u] = product(wh_q, t, half, "ha", 3)
            kept[u] = carry[(3, 0)] if u == (2, 1) else ring.tile([P, HALF], F32, name="kept")
            made[u] = carry[u] if t < 2 else ring.tile([P, HALF], F32, name="made")

        def keep_part(u, c0, w):
            t, half = u
            nc.vector.tensor_tensor(
                kept[u][:, c0 : c0 + w],
                r_sb[t][:].indirect(list_cols(half * HALF + c0, w)),
                carry[u][:, c0 : c0 + w],
                ALU.mult,
            )

        def make_part(u):
            nc.vector.scalar_tensor_tensor(made[u][:], ha[u][:], 0.0, gate[u][:], ALU.max, ALU.mult)

        def store_y(u):
            t, half = u
            nc.sync.dma_start(out_rows[:, t, half * HALF : (half + 1) * HALF], y[half][:, t, :])

        def add_on_vector(u, c0, w):
            t, half = u
            cols = slice(c0, c0 + w)
            nc.vector.tensor_tensor(y[half][:, t, cols], kept[u][:, cols], made[u][:, cols], ALU.add)

        def add_on_tensor(u, first):
            bank = psum.tile([P, HALF], F32, name="turn", bufs=3)
            for c0 in range(first, HALF, P):
                cols = slice(c0, c0 + P)
                nc.tensor.matmul(bank[:, cols], made[u][:, cols], ident[:], start=True, stop=False, is_transpose=True)
                nc.tensor.matmul(bank[:, cols], kept[u][:, cols], ident[:], start=False, stop=True, is_transpose=True)
            turned[u] = ring.tile([P, HALF], F32, name="turned", bufs=3)
            nc.scalar.copy(turned[u][:, first:], bank[:, first:])

        def turn_back(u, first):
            t, half = u
            bank = psum.tile([P, HALF], F32, name="turn", bufs=3)
            for c0 in range(first, HALF, P):
                cols = slice(c0, c0 + P)
                nc.tensor.transpose(bank[:, cols], turned[u][:, cols], ident[:])
            nc.scalar.copy(y[half][:, t, first:], bank[:, first:])
            store_y(u)

        def round_y(copy, half, c0, w):
            rounded = keep.tile([P, PACK * w], BF16, name="rounded%d" % (half * HALF + c0), align_bytes=64)
            copy(
                rounded[:].rearrange("p (c e t) -> p c t e", e=4, t=PACK),
                y[half][:, :, c0 : c0 + w].rearrange("p t (c e) -> p c t e", e=4),
            )
            return rounded

        def quantize_y(rounded, half, c0, w):
            j0 = half * HALF + c0
            nc.vector.quantize_mx(
                out=y_codes[:, j0 : j0 + w].bitcast(FP8X4),
                scales=y_scales[:, j0 : j0 + w],
                in_=rounded[:],
            )

        def store_codes(j0, w):
            nc.sync.dma_start(out_words[:, j0 : j0 + w], y_codes[:, j0 : j0 + w].bitcast(I32))

        def terms(u):
            gates(u)
            keep_part(u, 0, HALF)
            make_part(u)

        for u in [(0, 0), (0, 1), (1, 0), (1, 1), (2, 0)]:
            terms(u)
        add_on_tensor((0, 0), 0)
        add_on_tensor((0, 1), 0)
        gates((3, 0))
        keep_part((3, 0), 0, HALF)
        add_on_vector((2, 0), 0, QUARTER)
        make_part((3, 0))
        turn_back((0, 0), 0)
        turn_back((0, 1), 0)
        add_on_tensor((1, 0), 0)

        u2, u3 = (2, 1), (3, 1)
        gates(u2)
        add_on_tensor((1, 1), 0)
        turn_back((1, 0), 0)
        add_on_tensor((2, 0), QUARTER)
        gates(u3)
        turn_back((2, 0), QUARTER)
        turn_back((1, 1), 0)
        keep_part(u2, 0, QUARTER)
        add_on_vector((3, 0), 0, HALF)
        store_y((3, 0))
        first_half = round_y(nc.scalar.copy, 0, 0, HALF)
        make_part(u2)
        keep_part(u3, 0, QUARTER)
        make_part(u3)
        add_on_vector(u2, 0, QUARTER)
        add_on_vector(u3, 0, QUARTER)
        third = round_y(nc.scalar.copy, 1, 0, QUARTER)
        keep_part(u2, QUARTER, QUARTER)
        quantize_y(first_half, 0, 0, HALF)
        store_codes(0, HALF)
        keep_part(u3, QUARTER, QUARTER)
        add_on_vector(u2, QUARTER, QUARTER)
        store_y(u2)
        add_on_vector(u3, QUARTER, QUARTER)
        store_y(u3)
        eighth = QUARTER // 2
        by_scalar = round_y(nc.scalar.copy, 1, QUARTER, eighth)
        quantize_y(third, 1, 0, QUARTER)
        store_codes(HALF, QUARTER)
        by_vector = round_y(nc.vector.tensor_copy, 1, QUARTER + eighth, eighth)
        quantize_y(by_scalar, 1, QUARTER, eighth)
        quantize_y(by_vector, 1, QUARTER + eighth, eighth)
        store_codes(HALF + QUARTER, QUARTER)

        for q in range(4):
            queue = nc.scalar if q % 2 else nc.sync
            queue.dma_start(
                out_2[0, 4 * q : 4 * q + 4, :].bitcast(I32),
                y_scales[32 * q : 32 * q + 4, :].bitcast(I32),
            )
